import numpy as np
import ml_dtypes


def mxq(x, axis, fmt="e4m3"):
    dtype, down = {"e4m3": (ml_dtypes.float8_e4m3fn, 7), "e5m2": (ml_dtypes.float8_e5m2, 14)}[fmt]
    v = np.moveaxis(np.asarray(x, np.float32).astype(ml_dtypes.bfloat16).astype(np.float64), axis, -1)
    blocks = v.reshape(v.shape[:-1] + (-1, 32))
    amax = np.abs(blocks).max(-1, keepdims=True)
    byte = np.maximum(np.where(amax > 0, np.frexp(amax)[1] - 1 + 127, 0) - down, 1)
    scale = np.exp2(byte - 127.0)
    codes = (blocks / scale).astype(np.float32).astype(dtype).astype(np.float64)
    return np.moveaxis((codes * scale).reshape(v.shape), -1, axis)


WIDE = False


def mx_kscale(k):
    if not WIDE:
        return np.ones(k)
    levels = np.array([10, -10, 5, -5, 0])
    if k % 512:
        return np.exp2(np.random.permutation(np.resize(levels, k // 32))).repeat(32)
    a = np.empty((k // 512, 16))
    for p in range(k // 512):
        a[p, :8] = np.random.permutation(np.resize(levels, 8))
        for g in range(8):
            far = levels[np.abs(levels - a[p, g]) >= 10]
            a[p, g + 8] = far[np.random.randint(len(far))]
    return np.exp2(a.ravel()).repeat(32)


def f64(x):
    return np.asarray(x).astype(np.float64)


def striped(idx):
    return np.tile(idx.reshape(-1, 16).T, (8, 1)).astype(np.uint16)


def unstriped(offs):
    return offs[:16].T.reshape(-1).astype(np.int64)


def pack_weight(w):
    k, n = w.shape
    w = f64(np.asarray(w, np.float32).astype(ml_dtypes.bfloat16)).reshape(k // 32, 32, n)
    amax = np.abs(w).max(1)
    byte = np.clip(np.where(amax > 0, np.frexp(amax)[1] - 1 + 127 - 7, 1), 1, 254)
    scaled = (w * np.exp2(127.0 - byte)[:, None, :]).reshape(k, n).astype(np.float32)
    words = np.ascontiguousarray(scaled.reshape(k // 512, 128, 4, n).transpose(0, 1, 3, 2)).astype(ml_dtypes.float8_e4m3fn).view(np.uint8)
    return words, np.ascontiguousarray(byte.astype(np.uint8).reshape(k // 512, 16, n))


def unpack_weight(words, scales):
    g, p, n, _ = words.shape
    vals = np.ascontiguousarray(words).view(ml_dtypes.float8_e4m3fn).astype(np.float64) * np.repeat(np.exp2(scales.astype(np.float64) - 127.0), 8, axis=1)[..., None]
    return vals.transpose(0, 1, 3, 2).reshape(g * 512, n)


def relu(v):
    return np.maximum(v, 0.0)


K, T, S, V, W, U = 512, 1024, 512, 256, 2048, 1024
P = 2 ** 7


def setup_inputs():
    n = np.random.standard_normal
    s = mx_kscale(K)[:, None]
    packed_xT = pack_weight(n((K, T)) * s)
    packed_eT = pack_weight(n((K, W)) * s)
    return {
        "x_words": packed_xT[0],
        "x_scales": packed_xT[1],
        "e_words": packed_eT[0],
        "e_scales": packed_eT[1],
        "wq": (n((K, V)) / np.sqrt(K) / s).astype(np.float32),
        "wt": (n((K, V)) / np.sqrt(K) / s).astype(np.float32),
        "disc": (np.random.uniform(0.7, 1.0, (S, 1))).astype(np.float32),
        "rew": (n((S, 1))).astype(np.float32),
        "tau": (np.tile(np.random.uniform(0.05, 0.95, U), (P, 1))).astype(np.float32),
        "ku": (np.tile(np.random.uniform(0.8, 1.2, U), (P, 1))).astype(np.float32),
        "kd": (np.tile(np.random.uniform(0.8, 1.2, U), (P, 1))).astype(np.float32),
        "offs": striped(np.random.permutation(T)[:S]),
        "nxt": striped(np.random.permutation(W)[:S]),
        "pa": striped(np.random.permutation(np.concatenate([np.arange(V), np.random.randint(0, V, U - V)]))),
        "pb": striped(np.random.permutation(np.concatenate([np.arange(V), np.random.randint(0, V, U - V)]))),
    }


def reference(x_words, x_scales, e_words, e_scales, wq, wt, disc, rew, tau, ku, kd, offs, nxt, pa, pb):
    e_nxt = unpack_weight(e_words, e_scales)[:, unstriped(nxt)]
    wtq = mxq(f64(wt), 0, "e4m3")
    h = f64(disc) * (e_nxt.T @ wtq) + f64(rew)
    xq = unpack_weight(x_words, x_scales)[:, unstriped(offs)]
    wqq = mxq(f64(wq), 0, "e4m3")
    y = xq.T @ wqq
    td = h[:, unstriped(pb)] - y[:, unstriped(pa)]
    up = relu(td)
    cu = np.minimum(up, f64(ku)[:1])
    dn = relu(-1.0 * td)
    cd = np.minimum(dn, f64(kd)[:1])
    ls = f64(tau)[:1] * (cu * (up - (0.5 * cu))) + cd * (dn - (0.5 * cd)) - (f64(tau)[:1] * (cd * (dn - (0.5 * cd))))
    return ls.reshape(len(ls), -1, 4).mean(axis=2)

@@ -1,0 +1,246 @@
+from contextlib import ExitStack
+
+import concourse.mybir as mybir
+from concourse.masks import make_identity
+
+F32 = mybir.dt.float32
+BF16 = mybir.dt.bfloat16
+I32 = mybir.dt.int32
+U32 = mybir.dt.uint32
+U16 = mybir.dt.uint16
+U8 = mybir.dt.uint8
+FP8X4 = mybir.dt.float8_e4m3fn_x4
+ALU = mybir.AluOpType
+ACT = mybir.ActivationFunctionType
+
+P = 128
+PACK = 4
+K = 512
+S = 512
+V = 256
+U = 1024
+RUN = 4
+HALF = 512
+TILES = S // P
+WINDOW = 520
+TINY = 1e-30
+
+FLOPS = 2 * 2 * S * K * V
+
+STAGES = [(0, (0, 1)), (1, (0, 1)), (0, (2, 3)), (1, (2,)), (1, (3,))]
+
+
+def tile_picked_yqrdqn_loss_p_kernel(tc, x_words, x_scales, e_words, e_scales, wq, wt, disc, rew, tau, ku, kd, offs, nxt, pa, pb, out):
+    nc = tc.nc
+    with ExitStack() as ctx:
+        keep = ctx.enter_context(tc.tile_pool(name="keep", bufs=1))
+        work = ctx.enter_context(tc.tile_pool(name="work", bufs=4))
+        psum = ctx.enter_context(tc.psum_pool(name="psum", bufs=4))
+
+        def load_list(name, src):
+            t = keep.tile(list(src.shape), U16, name=name)
+            nc.sync.dma_start(t[:], src)
+            return t
+
+        def scale_table(name, src):
+            t = keep.tile([P, src.shape[2]], U8, name=name, align_bytes=64)
+            nc.vector.memset(t[:].bitcast(I32), 0)
+            return t
+
+        def load_scales(t, src):
+            for q in range(4):
+                nc.sync.dma_start(t[32 * q : 32 * q + 4, :].bitcast(I32), src[0, 4 * q : 4 * q + 4, :].bitcast(I32))
+
+        def load_words(name, src):
+            t = keep.tile([P, src.shape[2]], I32, name=name, align_bytes=64)
+            nc.sync.dma_start(t[:], src[0].rearrange("p n t -> p (n t)").bitcast(I32))
+            return t
+
+        def load_weight(name, src):
+            t = keep.tile([P, PACK, V], F32, name=name, align_bytes=64)
+            nc.sync.dma_start(t[:], src.rearrange("(p j) v -> p j v", j=PACK))
+            return t
+
+        def pair_row(src):
+            return src[0:1, :].rearrange("o (h p d) -> p (o h) d", h=2, d=RUN)
+
+        n = 2 * RUN
+        tau_sb = keep.tile([P, 2, RUN], F32, name="tau_sb")
+        kd_sb = keep.tile([P, 2, RUN], F32, name="kd_sb")
+        bound = keep.tile([P, 2 * n], F32, name="bound")
+        nc.gpsimd.dma_start(tau_sb[:], pair_row(tau))
+        nc.gpsimd.dma_start(kd_sb[:], pair_row(kd))
+        nc.gpsimd.dma_start(bound[:, 0:n].rearrange("p (h d) -> p h d", d=RUN), pair_row(ku))
+
+        xs_tab = scale_table("xs_tab", x_scales)
+        es_tab = scale_table("es_tab", e_scales)
+        offs_sb = load_list("offs_sb", offs)
+        load_scales(xs_tab, x_scales)
+        wq_raw = load_weight("wq_raw", wq)
+        xw_tab = load_words("xw_tab", x_words)
+        nxt_sb = load_list("nxt_sb", nxt)
+        load_scales(es_tab, e_scales)
+        wt_raw = load_weight("wt_raw", wt)
+        pa_sb = load_list("pa_sb", pa)
+        ew_tab = load_words("ew_tab", e_words)
+        pb_sb = load_list("pb_sb", pb)
+        disc_sb = keep.tile([P, TILES], F32, name="disc_sb")
+        rew_sb = keep.tile([P, TILES], F32, name="rew_sb")
+        with nc.allow_non_contiguous_dma(reason="one value a partition"):
+            nc.sync.dma_start(disc_sb[:], disc.rearrange("(i p) o -> p (i o)", p=P))
+            nc.sync.dma_start(rew_sb[:], rew.rearrange("(i p) o -> p (i o)", p=P))
+
+        power = keep.tile([P, 3 * n], F32, name="power")
+        nc.gpsimd.memset(power[:, 0 : 2 * n], 0.5)
+        nc.gpsimd.memset(power[:, 2 * n : 3 * n], -0.5)
+        ident = keep.tile([P, P], F32, name="ident")
+        make_identity(nc, ident[:])
+
+        tau_f = tau_sb[:].rearrange("p h d -> p (h d)")
+        kd_f = kd_sb[:].rearrange("p h d -> p (h d)")
+        curve = keep.tile([P, 3 * n], F32, name="curve")
+        nc.scalar.activation(curve[:, 0:n], tau_f, ACT.Copy, scale=0.125, bias=TINY)
+        nc.scalar.activation(curve[:, n : 2 * n], tau_f, ACT.Copy, scale=-0.125, bias=0.125)
+        nc.scalar.activation(curve[:, 2 * n : 3 * n], tau_f, ACT.Copy, scale=0.125, bias=TINY)
+        nc.scalar.activation(bound[:, n : 2 * n], kd_f, ACT.Copy, scale=-1.0)
+        root = keep.tile([P, 3 * n], F32, name="root")
+        nc.gpsimd.tensor_tensor(root[:], curve[:], power[:], ALU.pow)
+        slope = keep.tile([P, 2 * n], F32, name="slope")
+        nc.vector.scalar_tensor_tensor(slope[:], curve[:, 0 : 2 * n], 2.0, bound[:], ALU.mult, ALU.mult)
+        shift = keep.tile([P, 2 * n], F32, name="shift")
+        nc.vector.scalar_tensor_tensor(shift[:], slope[:], -1.0, bound[:], ALU.mult, ALU.mult)
+        ratio = keep.tile([P, n], F32, name="ratio")
+        nc.vector.scalar_tensor_tensor(ratio[:], root[:, n : 2 * n], -1.0, root[:, 2 * n : 3 * n], ALU.mult, ALU.mult)
+
+        def gather_bytes(name, table, lst, lo, hi):
+            t = keep.tile([P, hi - lo], U8, name=name, align_bytes=64)
+            nc.vector.tensor_copy(t[:], table[:].indirect(lst[:, lo // 16 : hi // 16]))
+            return t
+
+        def gather_words(name, table, lst, lo, hi):
+            t = keep.tile([P, hi - lo], U32, name=name, align_bytes=64)
+            nc.vector.tensor_copy(t[:], table[:].bitcast(U32).indirect(lst[:, lo // 16 : hi // 16]))
+            return t
+
+        def interleave(name, raw):
+            grouped = keep.tile([P, V, PACK], BF16, name=name, align_bytes=64)
+            nc.scalar.copy(
+                grouped[:].rearrange("p (c i) j -> p c j i", i=4),
+                raw[:].rearrange("p j (c i) -> p c j i", i=4),
+            )
+            return grouped
+
+        def quantise(name, grouped):
+            codes = keep.tile([P, V], U32, name=name + "_codes", align_bytes=64)
+            scales = keep.tile([P, V], U8, name=name + "_scales", align_bytes=64)
+            nc.vector.quantize_mx(codes[:].bitcast(FP8X4), scales[:], grouped[:].rearrange("p v j -> p (v j)"))
+            return codes, scales
+
+        def product(words, scales, w, first):
+            acc = psum.tile([P, 2, V], F32, name="acc", tag="acc")
+            for s in range(2):
+                cols = slice((first + s) * P, (first + s + 1) * P)
+                nc.tensor.matmul_mx(
+                    acc[:, s, :], words[:, cols].bitcast(FP8X4), scales[:, cols],
+                    w[0][:].bitcast(FP8X4), w[1][:], start=True, stop=True,
+                )
+            return acc
+
+        y_neg = [keep.tile([P, WINDOW], F32, name=f"y_neg{i}") for i in range(TILES)]
+        h_sb = [keep.tile([P, WINDOW], F32, name=f"h_sb{i}") for i in range(TILES)]
+        res = [keep.tile([P, V], F32, name=f"res{i}") for i in range(TILES)]
+
+        def targets(g, words, scales, w):
+            acc = product(words, scales, w, 0)
+            for s in range(2):
+                i = 2 * g + s
+                nc.scalar.activation(h_sb[i][:, 0:V], acc[:, s, :], ACT.Identity,
+                                     bias=rew_sb[:, i : i + 1], scale=disc_sb[:, i : i + 1])
+
+        picked_y = {}
+        td = {}
+
+        def fetch_y(stage):
+            half, tiles = stage
+            for i in tiles:
+                t = keep.tile([P, HALF], F32, name=f"yg{half}_{i}")
+                nc.vector.tensor_copy(t[:], y_neg[i][:].indirect(pa_sb[:, 32 * half : 32 * (half + 1)]))
+                picked_y[half, i] = t
+
+        def fetch_h(stage):
+            half, tiles = stage
+            for i in tiles:
+                t = keep.tile([P, HALF], F32, name=f"td{half}_{i}")
+                nc.vector.tensor_tensor(t[:], h_sb[i][:].indirect(pb_sb[:, 32 * half : 32 * (half + 1)]),
+                                        picked_y[half, i][:], ALU.add)
+                td[half, i] = t
+
+        def turn(stage):
+            half, tiles = stage
+            width = P * len(tiles)
+            per_bank = HALF // width
+            turned = []
+            for d0 in range(0, RUN, per_bank):
+                bank = psum.tile([P, HALF], F32, name="bank", tag="bank")
+                for d in range(d0, d0 + per_bank):
+                    for s, i in enumerate(tiles):
+                        at = (d - d0) * width + s * P
+                        nc.tensor.transpose(bank[:, at : at + P], td[half, i][:, d:HALF:RUN], ident[:])
+                x = work.tile([P, HALF], F32, name="x")
+                nc.scalar.copy(x[:], bank[:])
+                for d in range(d0, d0 + per_bank):
+                    turned.append(x[:, (d - d0) * width : (d - d0 + 1) * width])
+            return turned
+
+        def loss(stage, turned):
+            half, tiles = stage
+            width = P * len(tiles)
+            terms = []
+            clipped = []
+            for d in range(RUN):
+                j = RUN * half + d
+                c = work.tile([P, width], F32, name="c", bufs=8)
+                nc.vector.tensor_scalar(c[:], turned[d], bound[:, j : j + 1], bound[:, n + j : n + j + 1], ALU.min, ALU.max)
+                clipped.append(c)
+                for side in range(2):
+                    t = work.tile([P, width], F32, name="lin", bufs=16)
+                    col = slice(side * n + j, side * n + j + 1)
+                    nc.scalar.activation(t[:], turned[d], ACT.Relu, bias=shift[:, col], scale=slope[:, col])
+                    terms.append(t)
+            for d in range(RUN):
+                j = RUN * half + d
+                m = work.tile([P, width], F32, name="m", bufs=8)
+                nc.vector.scalar_tensor_tensor(m[:], clipped[d][:], ratio[:, j : j + 1], clipped[d][:], ALU.mult, ALU.max)
+                t = work.tile([P, width], F32, name="sq", bufs=8)
+                nc.scalar.activation(t[:], m[:], ACT.Square, scale=root[:, j : j + 1])
+                terms.append(t)
+            for s, i in enumerate(tiles):
+                total = psum.tile([P, P], F32, name="total", tag="acc")
+                for at, t in enumerate(terms):
+                    nc.tensor.matmul(total[:], t[:, s * P : (s + 1) * P], ident[:], is_transpose=True,
+                                     start=(at == 0), stop=(at == len(terms) - 1))
+                nc.scalar.copy(res[i][:, half * P : (half + 1) * P], total[:])
+                if half == 1:
+                    nc.sync.dma_start(out[i * P : (i + 1) * P, :], res[i][:])
+
+        x_bytes = gather_bytes("x_bytes", xs_tab, offs_sb, 0, S)
+        x_codes = gather_words("x_codes", xw_tab, offs_sb, 0, S)
+        wq_mx = quantise("wq", interleave("wq_grouped", wq_raw))
+        for g in range(2):
+            acc = product(x_codes, x_bytes, wq_mx, 2 * g)
+            for s in range(2):
+                nc.scalar.activation(y_neg[2 * g + s][:, 0:V], acc[:, s, :], ACT.Copy, scale=-1.0)
+        e_bytes = [gather_bytes(f"e_bytes{g}", es_tab, nxt_sb, g * V, (g + 1) * V) for g in range(2)]
+        wt_mx = quantise("wt", interleave("wt_grouped", wt_raw))
+        targets(0, gather_words("e_codes0", ew_tab, nxt_sb, 0, V), e_bytes[0], wt_mx)
+        fetch_y(STAGES[0])
+        fetch_h(STAGES[0])
+        turned = turn(STAGES[0])
+        targets(1, gather_words("e_codes1", ew_tab, nxt_sb, V, S), e_bytes[1], wt_mx)
+        for k, stage in enumerate(STAGES):
+            if k + 1 < len(STAGES):
+                fetch_y(STAGES[k + 1])
+                fetch_h(STAGES[k + 1])
+                ahead = turn(STAGES[k + 1])
+            loss(stage, turned)
+            turned = ahead

@@ -27,7 +27,7 @@ TINY = 1e-30
 
 FLOPS = 2 * 2 * S * K * V
 
-STAGES = [(0, (0, 1)), (1, (0, 1)), (0, (2, 3)), (1, (2,)), (1, (3,))]
+STAGES = [(0, (0,)), (0, (1,)), (1, (0, 1)), (0, (2, 3)), (1, (2,)), (1, (3,))]
 
 
 def tile_picked_yqrdqn_loss_p_kernel(tc, x_words, x_scales, e_words, e_scales, wq, wt, disc, rew, tau, ku, kd, offs, nxt, pa, pb, out):
@@ -44,7 +44,7 @@ def tile_picked_yqrdqn_loss_p_kernel(tc, x_words, x_scales, e_words, e_scales, w
 
         def scale_table(name, src):
             t = keep.tile([P, src.shape[2]], U8, name=name, align_bytes=64)
-            nc.vector.memset(t[:].bitcast(I32), 0)
+            nc.gpsimd.memset(t[:].bitcast(I32), 0)
             return t
 
         def load_scales(t, src):
@@ -65,52 +65,54 @@ def tile_picked_yqrdqn_loss_p_kernel(tc, x_words, x_scales, e_words, e_scales, w
             return src[0:1, :].rearrange("o (h p d) -> p (o h) d", h=2, d=RUN)
 
         n = 2 * RUN
+        xs_tab = scale_table("xs_tab", x_scales)
+        es_tab = scale_table("es_tab", e_scales)
         tau_sb = keep.tile([P, 2, RUN], F32, name="tau_sb")
         kd_sb = keep.tile([P, 2, RUN], F32, name="kd_sb")
         bound = keep.tile([P, 2 * n], F32, name="bound")
-        nc.gpsimd.dma_start(tau_sb[:], pair_row(tau))
-        nc.gpsimd.dma_start(kd_sb[:], pair_row(kd))
-        nc.gpsimd.dma_start(bound[:, 0:n].rearrange("p (h d) -> p h d", d=RUN), pair_row(ku))
-
-        xs_tab = scale_table("xs_tab", x_scales)
-        es_tab = scale_table("es_tab", e_scales)
-        offs_sb = load_list("offs_sb", offs)
-        load_scales(xs_tab, x_scales)
-        wq_raw = load_weight("wq_raw", wq)
-        xw_tab = load_words("xw_tab", x_words)
-        nxt_sb = load_list("nxt_sb", nxt)
-        load_scales(es_tab, e_scales)
-        wt_raw = load_weight("wt_raw", wt)
-        pa_sb = load_list("pa_sb", pa)
-        ew_tab = load_words("ew_tab", e_words)
-        pb_sb = load_list("pb_sb", pb)
         disc_sb = keep.tile([P, TILES], F32, name="disc_sb")
         rew_sb = keep.tile([P, TILES], F32, name="rew_sb")
+
+        nc.sync.dma_start(tau_sb[:], pair_row(tau))
+        offs_sb = load_list("offs_sb", offs)
+        load_scales(xs_tab, x_scales)
+        xw_tab = load_words("xw_tab", x_words)
+        wq_raw = load_weight("wq_raw", wq)
+        load_scales(es_tab, e_scales)
+        nxt_sb = load_list("nxt_sb", nxt)
+        wt_raw = load_weight("wt_raw", wt)
+        ew_tab = load_words("ew_tab", e_words)
+        pb_sb = load_list("pb_sb", pb)
         with nc.allow_non_contiguous_dma(reason="one value a partition"):
             nc.sync.dma_start(disc_sb[:], disc.rearrange("(i p) o -> p (i o)", p=P))
             nc.sync.dma_start(rew_sb[:], rew.rearrange("(i p) o -> p (i o)", p=P))
+        pa_sb = load_list("pa_sb", pa)
+        nc.sync.dma_start(bound[:, 0:n].rearrange("p (h d) -> p h d", d=RUN), pair_row(ku))
+        nc.sync.dma_start(kd_sb[:], pair_row(kd))
 
-        power = keep.tile([P, 3 * n], F32, name="power")
-        nc.gpsimd.memset(power[:, 0 : 2 * n], 0.5)
-        nc.gpsimd.memset(power[:, 2 * n : 3 * n], -0.5)
         ident = keep.tile([P, P], F32, name="ident")
         make_identity(nc, ident[:])
 
         tau_f = tau_sb[:].rearrange("p h d -> p (h d)")
         kd_f = kd_sb[:].rearrange("p h d -> p (h d)")
-        curve = keep.tile([P, 3 * n], F32, name="curve")
-        nc.scalar.activation(curve[:, 0:n], tau_f, ACT.Copy, scale=0.125, bias=TINY)
-        nc.scalar.activation(curve[:, n : 2 * n], tau_f, ACT.Copy, scale=-0.125, bias=0.125)
-        nc.scalar.activation(curve[:, 2 * n : 3 * n], tau_f, ACT.Copy, scale=0.125, bias=TINY)
-        nc.scalar.activation(bound[:, n : 2 * n], kd_f, ACT.Copy, scale=-1.0)
-        root = keep.tile([P, 3 * n], F32, name="root")
-        nc.gpsimd.tensor_tensor(root[:], curve[:], power[:], ALU.pow)
-        slope = keep.tile([P, 2 * n], F32, name="slope")
-        nc.vector.scalar_tensor_tensor(slope[:], curve[:, 0 : 2 * n], 2.0, bound[:], ALU.mult, ALU.mult)
-        shift = keep.tile([P, 2 * n], F32, name="shift")
-        nc.vector.scalar_tensor_tensor(shift[:], slope[:], -1.0, bound[:], ALU.mult, ALU.mult)
+        root = keep.tile([P, n], F32, name="root")
+        nc.scalar.activation(root[:], tau_f, ACT.Sqrt, scale=0.125, bias=TINY)
+        weight = keep.tile([P, 2 * n], F32, name="weight")
+        nc.scalar.activation(weight[:, n : 2 * n], tau_f, ACT.Copy, scale=-0.25, bias=0.25)
+        nc.scalar.activation(weight[:, 0:n], tau_f, ACT.Copy, scale=0.25)
+        root_dn = keep.tile([P, n], F32, name="root_dn")
+        nc.scalar.activation(root_dn[:], weight[:, n : 2 * n], ACT.Sqrt, scale=0.5, bias=TINY)
+        inverse = keep.tile([P, n], F32, name="inverse")
+        nc.vector.reciprocal(inverse[:], root[:])
         ratio = keep.tile([P, n], F32, name="ratio")
-        nc.vector.scalar_tensor_tensor(ratio[:], root[:, n : 2 * n], -1.0, root[:, 2 * n : 3 * n], ALU.mult, ALU.mult)
+        nc.vector.scalar_tensor_tensor(ratio[:], root_dn[:], -1.0, inverse[:], ALU.mult, ALU.mult)
+        nc.gpsimd.tensor_scalar(bound[:, n : 2 * n], kd_f, -1.0, 0.0, ALU.mult, ALU.add)
+        slope = keep.tile([P, 2 * n], F32, name="slope")
+        nc.gpsimd.tensor_tensor(slope[:], weight[:], bound[:], ALU.mult)
+        knee = keep.tile([P, 2 * n], F32, name="knee")
+        nc.gpsimd.tensor_tensor(knee[:], slope[:], bound[:], ALU.mult)
+        shift = keep.tile([P, 2 * n], F32, name="shift")
+        nc.gpsimd.tensor_scalar(shift[:], knee[:], -1.0, 0.0, ALU.mult, ALU.add)
 
         def gather_bytes(name, table, lst, lo, hi):
             t = keep.tile([P, hi - lo], U8, name=name, align_bytes=64)
@@ -159,18 +161,19 @@ def tile_picked_yqrdqn_loss_p_kernel(tc, x_words, x_scales, e_words, e_scales, w
 
         picked_y = {}
         td = {}
+        ring = [[keep.tile([P, HALF], F32, name=f"ring{a}_{s}") for s in range(2)] for a in range(2)]
 
         def fetch_y(stage):
             half, tiles = stage
             for i in tiles:
-                t = keep.tile([P, HALF], F32, name=f"yg{half}_{i}")
+                t = work.tile([P, HALF], F32, name="yg", bufs=2)
                 nc.vector.tensor_copy(t[:], y_neg[i][:].indirect(pa_sb[:, 32 * half : 32 * (half + 1)]))
                 picked_y[half, i] = t
 
         def fetch_h(stage):
             half, tiles = stage
-            for i in tiles:
-                t = keep.tile([P, HALF], F32, name=f"td{half}_{i}")
+            for s, i in enumerate(tiles):
+                t = ring[STAGES.index(stage) % 2][s]
                 nc.vector.tensor_tensor(t[:], h_sb[i][:].indirect(pb_sb[:, 32 * half : 32 * (half + 1)]),
                                         picked_y[half, i][:], ALU.add)
                 td[half, i] = t
@@ -199,8 +202,9 @@ def tile_picked_yqrdqn_loss_p_kernel(tc, x_words, x_scales, e_words, e_scales, w
             clipped = []
             for d in range(RUN):
                 j = RUN * half + d
-                c = work.tile([P, width], F32, name="c", bufs=8)
-                nc.vector.tensor_scalar(c[:], turned[d], bound[:, j : j + 1], bound[:, n + j : n + j + 1], ALU.min, ALU.max)
+                at = d * width
+                c = td[half, tiles[at // HALF]][:, at % HALF : at % HALF + width]
+                nc.vector.tensor_scalar(c, turned[d], bound[:, j : j + 1], bound[:, n + j : n + j + 1], ALU.min, ALU.max)
                 clipped.append(c)
                 for side in range(2):
                     t = work.tile([P, width], F32, name="lin", bufs=16)
@@ -210,7 +214,7 @@ def tile_picked_yqrdqn_loss_p_kernel(tc, x_words, x_scales, e_words, e_scales, w
             for d in range(RUN):
                 j = RUN * half + d
                 m = work.tile([P, width], F32, name="m", bufs=8)
-                nc.vector.scalar_tensor_tensor(m[:], clipped[d][:], ratio[:, j : j + 1], clipped[d][:], ALU.mult, ALU.max)
+                nc.vector.scalar_tensor_tensor(m[:], clipped[d], ratio[:, j : j + 1], clipped[d], ALU.mult, ALU.max)
                 t = work.tile([P, width], F32, name="sq", bufs=8)
                 nc.scalar.activation(t[:], m[:], ACT.Square, scale=root[:, j : j + 1])
                 terms.append(t)
@@ -235,12 +239,11 @@ def tile_picked_yqrdqn_loss_p_kernel(tc, x_words, x_scales, e_words, e_scales, w
         targets(0, gather_words("e_codes0", ew_tab, nxt_sb, 0, V), e_bytes[0], wt_mx)
         fetch_y(STAGES[0])
         fetch_h(STAGES[0])
-        turned = turn(STAGES[0])
+        turned = [turn(STAGES[0])]
         targets(1, gather_words("e_codes1", ew_tab, nxt_sb, V, S), e_bytes[1], wt_mx)
         for k, stage in enumerate(STAGES):
             if k + 1 < len(STAGES):
                 fetch_y(STAGES[k + 1])
                 fetch_h(STAGES[k + 1])
-                ahead = turn(STAGES[k + 1])
-            loss(stage, turned)
-            turned = ahead
+                turned.append(turn(STAGES[k + 1]))
+            loss(stage, turned[k])

@@ -18,19 +18,23 @@ PACK = 4
 K = 512
 S = 512
 V = 256
-U = 1024
 RUN = 4
 HALF = 512
+CONSTS = 2 * RUN
 TILES = S // P
+GROUP = 2 * P
+PER_LIST_COLUMN = 16
 WINDOW = 520
 TINY = 1e-30
 
 FLOPS = 2 * 2 * S * K * V
 
-STAGES = [(0, (0,)), (0, (1,)), (1, (0, 1)), (0, (2, 3)), (1, (2,)), (1, (3,))]
+STAGES = [(0, (0, 1)), (1, (0, 1)), (0, (2, 3)), (1, (2,)), (1, (3,))]
 
 
-def tile_picked_yqrdqn_loss_p_kernel(tc, x_words, x_scales, e_words, e_scales, wq, wt, disc, rew, tau, ku, kd, offs, nxt, pa, pb, out):
+def tile_picked_yqrdqn_loss_p_kernel(
+    tc, x_words, x_scales, e_words, e_scales, wq, wt, disc, rew, tau, ku, kd, offs, nxt, pa, pb, out
+):
     nc = tc.nc
     with ExitStack() as ctx:
         keep = ctx.enter_context(tc.tile_pool(name="keep", bufs=1))
@@ -38,212 +42,240 @@ def tile_picked_yqrdqn_loss_p_kernel(tc, x_words, x_scales, e_words, e_scales, w
         psum = ctx.enter_context(tc.psum_pool(name="psum", bufs=4))
 
         def load_list(name, src):
-            t = keep.tile(list(src.shape), U16, name=name)
-            nc.sync.dma_start(t[:], src)
-            return t
+            tile = keep.tile(list(src.shape), U16, name=name)
+            nc.sync.dma_start(tile[:], src)
+            return tile
 
-        def scale_table(name, src):
-            t = keep.tile([P, src.shape[2]], U8, name=name, align_bytes=64)
-            nc.gpsimd.memset(t[:].bitcast(I32), 0)
-            return t
+        def cleared_scale_table(name, src):
+            tile = keep.tile([P, src.shape[2]], U8, name=name, tag=name, align_bytes=64)
+            nc.gpsimd.memset(tile[:].bitcast(I32), 0)
+            return tile
 
-        def load_scales(t, src):
+        def load_scales(tile, src):
             for q in range(4):
-                nc.sync.dma_start(t[32 * q : 32 * q + 4, :].bitcast(I32), src[0, 4 * q : 4 * q + 4, :].bitcast(I32))
+                nc.sync.dma_start(tile[32 * q : 32 * q + 4, :].bitcast(I32), src[0, 4 * q : 4 * q + 4, :].bitcast(I32))
 
         def load_words(name, src):
-            t = keep.tile([P, src.shape[2]], I32, name=name, align_bytes=64)
-            nc.sync.dma_start(t[:], src[0].rearrange("p n t -> p (n t)").bitcast(I32))
-            return t
+            tile = keep.tile([P, src.shape[2]], I32, name=name, align_bytes=64)
+            nc.sync.dma_start(tile[:], src[0].rearrange("p n t -> p (n t)").bitcast(I32))
+            return tile
 
         def load_weight(name, src):
-            t = keep.tile([P, PACK, V], F32, name=name, align_bytes=64)
-            nc.sync.dma_start(t[:], src.rearrange("(p j) v -> p j v", j=PACK))
-            return t
+            tile = keep.tile([P, PACK, V], F32, name=name, align_bytes=64)
+            nc.sync.dma_start(tile[:], src.rearrange("(p j) v -> p j v", j=PACK))
+            return tile
 
         def pair_row(src):
             return src[0:1, :].rearrange("o (h p d) -> p (o h) d", h=2, d=RUN)
 
-        n = 2 * RUN
-        xs_tab = scale_table("xs_tab", x_scales)
-        es_tab = scale_table("es_tab", e_scales)
+        xs_tab = cleared_scale_table("xs_tab", x_scales)
+        es_tab = cleared_scale_table("es_tab", e_scales)
         tau_sb = keep.tile([P, 2, RUN], F32, name="tau_sb")
         kd_sb = keep.tile([P, 2, RUN], F32, name="kd_sb")
-        bound = keep.tile([P, 2 * n], F32, name="bound")
+        bound = keep.tile([P, 2 * CONSTS], F32, name="bound")
         disc_sb = keep.tile([P, TILES], F32, name="disc_sb")
         rew_sb = keep.tile([P, TILES], F32, name="rew_sb")
 
         nc.sync.dma_start(tau_sb[:], pair_row(tau))
         offs_sb = load_list("offs_sb", offs)
         load_scales(xs_tab, x_scales)
+        wt_raw = load_weight("wt_raw", wt)
         xw_tab = load_words("xw_tab", x_words)
         wq_raw = load_weight("wq_raw", wq)
-        load_scales(es_tab, e_scales)
         nxt_sb = load_list("nxt_sb", nxt)
-        wt_raw = load_weight("wt_raw", wt)
+        load_scales(es_tab, e_scales)
         ew_tab = load_words("ew_tab", e_words)
         pb_sb = load_list("pb_sb", pb)
-        with nc.allow_non_contiguous_dma(reason="one value a partition"):
+        with nc.allow_non_contiguous_dma(reason="transition 128 i + p goes to [p, i]"):
             nc.sync.dma_start(disc_sb[:], disc.rearrange("(i p) o -> p (i o)", p=P))
             nc.sync.dma_start(rew_sb[:], rew.rearrange("(i p) o -> p (i o)", p=P))
-        pa_sb = load_list("pa_sb", pa)
-        nc.sync.dma_start(bound[:, 0:n].rearrange("p (h d) -> p h d", d=RUN), pair_row(ku))
+        nc.sync.dma_start(bound[:, 0:CONSTS].rearrange("p (h d) -> p h d", d=RUN), pair_row(ku))
         nc.sync.dma_start(kd_sb[:], pair_row(kd))
+        pa_sb = load_list("pa_sb", pa)
 
         ident = keep.tile([P, P], F32, name="ident")
         make_identity(nc, ident[:])
 
         tau_f = tau_sb[:].rearrange("p h d -> p (h d)")
         kd_f = kd_sb[:].rearrange("p h d -> p (h d)")
-        root = keep.tile([P, n], F32, name="root")
-        nc.scalar.activation(root[:], tau_f, ACT.Sqrt, scale=0.125, bias=TINY)
-        weight = keep.tile([P, 2 * n], F32, name="weight")
-        nc.scalar.activation(weight[:, n : 2 * n], tau_f, ACT.Copy, scale=-0.25, bias=0.25)
-        nc.scalar.activation(weight[:, 0:n], tau_f, ACT.Copy, scale=0.25)
-        root_dn = keep.tile([P, n], F32, name="root_dn")
-        nc.scalar.activation(root_dn[:], weight[:, n : 2 * n], ACT.Sqrt, scale=0.5, bias=TINY)
-        inverse = keep.tile([P, n], F32, name="inverse")
-        nc.vector.reciprocal(inverse[:], root[:])
-        ratio = keep.tile([P, n], F32, name="ratio")
+        upper = slice(0, CONSTS)
+        lower = slice(CONSTS, 2 * CONSTS)
+        root_up = keep.tile([P, CONSTS], F32, name="root_up")
+        nc.scalar.activation(root_up[:], tau_f, ACT.Sqrt, scale=0.125, bias=TINY)
+        weight = keep.tile([P, 2 * CONSTS], F32, name="weight")
+        nc.scalar.activation(weight[:, lower], tau_f, ACT.Copy, scale=-0.25, bias=0.25)
+        nc.scalar.activation(weight[:, upper], tau_f, ACT.Copy, scale=0.25)
+        root_dn = keep.tile([P, CONSTS], F32, name="root_dn")
+        nc.scalar.activation(root_dn[:], weight[:, lower], ACT.Sqrt, scale=0.5, bias=TINY)
+        inverse = keep.tile([P, CONSTS], F32, name="inverse")
+        nc.vector.reciprocal(inverse[:], root_up[:])
+        ratio = keep.tile([P, CONSTS], F32, name="ratio")
         nc.vector.scalar_tensor_tensor(ratio[:], root_dn[:], -1.0, inverse[:], ALU.mult, ALU.mult)
-        nc.gpsimd.tensor_scalar(bound[:, n : 2 * n], kd_f, -1.0, 0.0, ALU.mult, ALU.add)
-        slope = keep.tile([P, 2 * n], F32, name="slope")
+        nc.gpsimd.tensor_scalar(bound[:, lower], kd_f, -1.0, 0.0, ALU.mult, ALU.add)
+        slope = keep.tile([P, 2 * CONSTS], F32, name="slope")
         nc.gpsimd.tensor_tensor(slope[:], weight[:], bound[:], ALU.mult)
-        knee = keep.tile([P, 2 * n], F32, name="knee")
+        knee = keep.tile([P, 2 * CONSTS], F32, name="knee")
         nc.gpsimd.tensor_tensor(knee[:], slope[:], bound[:], ALU.mult)
-        shift = keep.tile([P, 2 * n], F32, name="shift")
+        shift = keep.tile([P, 2 * CONSTS], F32, name="shift")
         nc.gpsimd.tensor_scalar(shift[:], knee[:], -1.0, 0.0, ALU.mult, ALU.add)
 
-        def gather_bytes(name, table, lst, lo, hi):
-            t = keep.tile([P, hi - lo], U8, name=name, align_bytes=64)
-            nc.vector.tensor_copy(t[:], table[:].indirect(lst[:, lo // 16 : hi // 16]))
-            return t
+        def entries(lst, first, count):
+            return lst[:, first // PER_LIST_COLUMN : (first + count) // PER_LIST_COLUMN]
 
-        def gather_words(name, table, lst, lo, hi):
-            t = keep.tile([P, hi - lo], U32, name=name, align_bytes=64)
-            nc.vector.tensor_copy(t[:], table[:].bitcast(U32).indirect(lst[:, lo // 16 : hi // 16]))
-            return t
+        def gather_bytes(name, table, lst):
+            tile = keep.tile([P, S], U8, name=name, align_bytes=64)
+            nc.vector.tensor_copy(tile[:], table[:].indirect(entries(lst, 0, S)))
+            return tile
 
-        def interleave(name, raw):
-            grouped = keep.tile([P, V, PACK], BF16, name=name, align_bytes=64)
+        def gather_words(name, table, lst, group):
+            tile = keep.tile([P, GROUP], U32, name=name, align_bytes=64)
+            nc.vector.tensor_copy(tile[:], table[:].bitcast(U32).indirect(entries(lst, group * GROUP, GROUP)))
+            return tile
+
+        def quantise(name, raw, home):
+            grouped = keep.tile([P, V, PACK], BF16, name=name + "_grouped", align_bytes=64)
             nc.scalar.copy(
                 grouped[:].rearrange("p (c i) j -> p c j i", i=4),
                 raw[:].rearrange("p j (c i) -> p c j i", i=4),
             )
-            return grouped
-
-        def quantise(name, grouped):
-            codes = keep.tile([P, V], U32, name=name + "_codes", align_bytes=64)
+            codes = keep.tile([P, V], U32, name=name + "_codes", tag=home, align_bytes=64)
             scales = keep.tile([P, V], U8, name=name + "_scales", align_bytes=64)
             nc.vector.quantize_mx(codes[:].bitcast(FP8X4), scales[:], grouped[:].rearrange("p v j -> p (v j)"))
             return codes, scales
 
-        def product(words, scales, w, first):
+        def product(words, scale_bytes, group, weights):
             acc = psum.tile([P, 2, V], F32, name="acc", tag="acc")
             for s in range(2):
-                cols = slice((first + s) * P, (first + s + 1) * P)
+                first = group * GROUP + s * P
                 nc.tensor.matmul_mx(
-                    acc[:, s, :], words[:, cols].bitcast(FP8X4), scales[:, cols],
-                    w[0][:].bitcast(FP8X4), w[1][:], start=True, stop=True,
+                    acc[:, s, :],
+                    words[:, s * P : (s + 1) * P].bitcast(FP8X4),
+                    scale_bytes[:, first : first + P],
+                    weights[0][:].bitcast(FP8X4),
+                    weights[1][:],
+                    start=True,
+                    stop=True,
                 )
             return acc
 
         y_neg = [keep.tile([P, WINDOW], F32, name=f"y_neg{i}") for i in range(TILES)]
         h_sb = [keep.tile([P, WINDOW], F32, name=f"h_sb{i}") for i in range(TILES)]
-        res = [keep.tile([P, V], F32, name=f"res{i}") for i in range(TILES)]
+        result = [keep.tile([P, V], F32, name=f"result{i}") for i in range(TILES)]
 
-        def targets(g, words, scales, w):
-            acc = product(words, scales, w, 0)
+        def predictions(group, words):
+            acc = product(words, x_bytes, group, wq_mx)
             for s in range(2):
-                i = 2 * g + s
-                nc.scalar.activation(h_sb[i][:, 0:V], acc[:, s, :], ACT.Identity,
-                                     bias=rew_sb[:, i : i + 1], scale=disc_sb[:, i : i + 1])
+                nc.scalar.activation(y_neg[2 * group + s][:, 0:V], acc[:, s, :], ACT.Copy, scale=-1.0)
 
-        picked_y = {}
-        td = {}
-        ring = [[keep.tile([P, HALF], F32, name=f"ring{a}_{s}") for s in range(2)] for a in range(2)]
+        def targets(group):
+            acc = product(gather_words(f"e_codes{group}", ew_tab, nxt_sb, group), e_bytes, group, wt_mx)
+            for s in range(2):
+                i = 2 * group + s
+                nc.scalar.activation(
+                    h_sb[i][:, 0:V], acc[:, s, :], ACT.Identity, bias=rew_sb[:, i : i + 1], scale=disc_sb[:, i : i + 1]
+                )
 
-        def fetch_y(stage):
-            half, tiles = stage
-            for i in tiles:
-                t = work.tile([P, HALF], F32, name="yg", bufs=2)
-                nc.vector.tensor_copy(t[:], y_neg[i][:].indirect(pa_sb[:, 32 * half : 32 * (half + 1)]))
-                picked_y[half, i] = t
+        shared = [keep.tile([P, HALF], F32, name=f"shared{s}") for s in range(2)]
+        swap = [[keep.tile([P, HALF], F32, name=f"swap{a}_{b}") for b in range(2)] for a in range(2)]
+        totals = {}
 
-        def fetch_h(stage):
-            half, tiles = stage
+        def part(tiles2, d, width):
+            return tiles2[d // 2][:, (d % 2) * width : (d % 2 + 1) * width]
+
+        def differences(k):
+            half, tiles = STAGES[k]
+            picked = []
             for s, i in enumerate(tiles):
-                t = ring[STAGES.index(stage) % 2][s]
-                nc.vector.tensor_tensor(t[:], h_sb[i][:].indirect(pb_sb[:, 32 * half : 32 * (half + 1)]),
-                                        picked_y[half, i][:], ALU.add)
-                td[half, i] = t
+                y_picked = shared[s] if k > 0 else work.tile([P, HALF], F32, name="y_first", bufs=2)
+                nc.vector.tensor_copy(y_picked[:], y_neg[i][:].indirect(entries(pa_sb, half * HALF, HALF)))
+                picked.append(y_picked)
+            td = []
+            for s, i in enumerate(tiles):
+                diff = work.tile([P, HALF], F32, name="diff")
+                nc.vector.tensor_tensor(
+                    diff[:], h_sb[i][:].indirect(entries(pb_sb, half * HALF, HALF)), picked[s][:], ALU.add
+                )
+                td.append(diff)
+            return td
 
-        def turn(stage):
-            half, tiles = stage
-            width = P * len(tiles)
-            per_bank = HALF // width
-            turned = []
-            for d0 in range(0, RUN, per_bank):
-                bank = psum.tile([P, HALF], F32, name="bank", tag="bank")
-                for d in range(d0, d0 + per_bank):
-                    for s, i in enumerate(tiles):
-                        at = (d - d0) * width + s * P
-                        nc.tensor.transpose(bank[:, at : at + P], td[half, i][:, d:HALF:RUN], ident[:])
-                x = work.tile([P, HALF], F32, name="x")
-                nc.scalar.copy(x[:], bank[:])
-                for d in range(d0, d0 + per_bank):
-                    turned.append(x[:, (d - d0) * width : (d - d0 + 1) * width])
-            return turned
+        def turn(k, td):
+            width = P * len(td)
+            for b in range(2):
+                bank = psum.tile([P, 2 * width], F32, name="bank", tag="bank")
+                for d in (2 * b, 2 * b + 1):
+                    for s, diff in enumerate(td):
+                        at = (d % 2) * width + s * P
+                        nc.tensor.transpose(bank[:, at : at + P], diff[:, d:HALF:RUN], ident[:])
+                nc.scalar.copy(swap[k % 2][b][:, 0 : 2 * width], bank[:])
 
-        def loss(stage, turned):
-            half, tiles = stage
+        def linear_terms(k):
+            half, tiles = STAGES[k]
             width = P * len(tiles)
             terms = []
-            clipped = []
             for d in range(RUN):
-                j = RUN * half + d
-                at = d * width
-                c = td[half, tiles[at // HALF]][:, at % HALF : at % HALF + width]
-                nc.vector.tensor_scalar(c, turned[d], bound[:, j : j + 1], bound[:, n + j : n + j + 1], ALU.min, ALU.max)
-                clipped.append(c)
                 for side in range(2):
-                    t = work.tile([P, width], F32, name="lin", bufs=16)
-                    col = slice(side * n + j, side * n + j + 1)
-                    nc.scalar.activation(t[:], turned[d], ACT.Relu, bias=shift[:, col], scale=slope[:, col])
-                    terms.append(t)
+                    term = work.tile([P, width], F32, name="linear", bufs=4 * RUN)
+                    j = side * CONSTS + RUN * half + d
+                    nc.scalar.activation(
+                        term[:], part(swap[k % 2], d, width), ACT.Relu, bias=shift[:, j : j + 1], scale=slope[:, j : j + 1]
+                    )
+                    terms.append(term)
+            return terms
+
+        def square_terms(k):
+            half, tiles = STAGES[k]
+            width = P * len(tiles)
             for d in range(RUN):
                 j = RUN * half + d
-                m = work.tile([P, width], F32, name="m", bufs=8)
-                nc.vector.scalar_tensor_tensor(m[:], clipped[d], ratio[:, j : j + 1], clipped[d], ALU.mult, ALU.max)
-                t = work.tile([P, width], F32, name="sq", bufs=8)
-                nc.scalar.activation(t[:], m[:], ACT.Square, scale=root[:, j : j + 1])
-                terms.append(t)
-            for s, i in enumerate(tiles):
-                total = psum.tile([P, P], F32, name="total", tag="acc")
-                for at, t in enumerate(terms):
-                    nc.tensor.matmul(total[:], t[:, s * P : (s + 1) * P], ident[:], is_transpose=True,
-                                     start=(at == 0), stop=(at == len(terms) - 1))
-                nc.scalar.copy(res[i][:, half * P : (half + 1) * P], total[:])
-                if half == 1:
-                    nc.sync.dma_start(out[i * P : (i + 1) * P, :], res[i][:])
+                nc.vector.tensor_scalar(
+                    part(shared, d, width), part(swap[k % 2], d, width),
+                    bound[:, j : j + 1], bound[:, CONSTS + j : CONSTS + j + 1], ALU.min, ALU.max,
+                )
+            terms = []
+            for d in range(RUN):
+                j = RUN * half + d
+                clipped = part(shared, d, width)
+                folded = part(swap[(k + 1) % 2], d, width)
+                nc.vector.scalar_tensor_tensor(folded, clipped, ratio[:, j : j + 1], clipped, ALU.mult, ALU.max)
+                term = work.tile([P, width], F32, name="square", bufs=2 * RUN)
+                nc.scalar.activation(term[:], folded, ACT.Square, scale=root_up[:, j : j + 1])
+                terms.append(term)
+            return terms
 
-        x_bytes = gather_bytes("x_bytes", xs_tab, offs_sb, 0, S)
-        x_codes = gather_words("x_codes", xw_tab, offs_sb, 0, S)
-        wq_mx = quantise("wq", interleave("wq_grouped", wq_raw))
-        for g in range(2):
-            acc = product(x_codes, x_bytes, wq_mx, 2 * g)
-            for s in range(2):
-                nc.scalar.activation(y_neg[2 * g + s][:, 0:V], acc[:, s, :], ACT.Copy, scale=-1.0)
-        e_bytes = [gather_bytes(f"e_bytes{g}", es_tab, nxt_sb, g * V, (g + 1) * V) for g in range(2)]
-        wt_mx = quantise("wt", interleave("wt_grouped", wt_raw))
-        targets(0, gather_words("e_codes0", ew_tab, nxt_sb, 0, V), e_bytes[0], wt_mx)
-        fetch_y(STAGES[0])
-        fetch_h(STAGES[0])
-        turned = [turn(STAGES[0])]
-        targets(1, gather_words("e_codes1", ew_tab, nxt_sb, V, S), e_bytes[1], wt_mx)
-        for k, stage in enumerate(STAGES):
+        def add_up(k, terms):
+            half, tiles = STAGES[k]
+            for s, i in enumerate(tiles):
+                if half == 0:
+                    totals[i] = psum.tile([P, V], F32, name="total", tag="acc")
+                for at, term in enumerate(terms):
+                    nc.tensor.matmul(
+                        totals[i][:, half * P : (half + 1) * P], term[:, s * P : (s + 1) * P], ident[:],
+                        is_transpose=True, start=(at == 0), stop=(at == len(terms) - 1),
+                    )
+
+        def store(k):
+            half, tiles = STAGES[k]
+            if half == 1:
+                for i in tiles:
+                    nc.scalar.copy(result[i][:], totals[i][:])
+                    nc.sync.dma_start(out[i * P : (i + 1) * P, :], result[i][:])
+
+        x_bytes = gather_bytes("x_bytes", xs_tab, offs_sb)
+        wt_mx = quantise("wt", wt_raw, "xs_tab")
+        x_codes = [gather_words(f"x_codes{group}", xw_tab, offs_sb, group) for group in range(2)]
+        e_bytes = gather_bytes("e_bytes", es_tab, nxt_sb)
+        wq_mx = quantise("wq", wq_raw, "es_tab")
+        for group in range(2):
+            predictions(group, x_codes[group])
+        targets(0)
+        td = differences(0)
+        targets(1)
+        for k in range(len(STAGES)):
+            turn(k, td)
+            linear = linear_terms(k)
             if k + 1 < len(STAGES):
-                fetch_y(STAGES[k + 1])
-                fetch_h(STAGES[k + 1])
-                turned.append(turn(STAGES[k + 1]))
-            loss(stage, turned[k])
+                td = differences(k + 1)
+            add_up(k, linear + square_terms(k))
+            if k > 0:
+                store(k - 1)
+        store(len(STAGES) - 1)

@@ -25,6 +25,7 @@ TILES = S // P
 GROUP = 2 * P
 PER_LIST_COLUMN = 16
 WINDOW = 520
+X_ROWS, E_ROWS = 0, 4
 TINY = 1e-30
 
 FLOPS = 2 * 2 * S * K * V
@@ -51,9 +52,9 @@ def tile_picked_yqrdqn_loss_p_kernel(
             nc.gpsimd.memset(tile[:].bitcast(I32), 0)
             return tile
 
-        def load_scales(tile, src):
-            for q in range(4):
-                nc.sync.dma_start(tile[32 * q : 32 * q + 4, :].bitcast(I32), src[0, 4 * q : 4 * q + 4, :].bitcast(I32))
+        def load_scales(tile, src, first):
+            for r in range(4):
+                nc.sync.dma_start(tile[first + r : P : 32, :].bitcast(I32), src[0, r:16:4, :].bitcast(I32))
 
         def load_words(name, src):
             tile = keep.tile([P, src.shape[2]], I32, name=name, align_bytes=64)
@@ -78,20 +79,20 @@ def tile_picked_yqrdqn_loss_p_kernel(
 
         nc.sync.dma_start(tau_sb[:], pair_row(tau))
         offs_sb = load_list("offs_sb", offs)
-        load_scales(xs_tab, x_scales)
+        load_scales(xs_tab, x_scales, X_ROWS)
         wt_raw = load_weight("wt_raw", wt)
         xw_tab = load_words("xw_tab", x_words)
-        wq_raw = load_weight("wq_raw", wq)
         nxt_sb = load_list("nxt_sb", nxt)
-        load_scales(es_tab, e_scales)
+        load_scales(es_tab, e_scales, E_ROWS)
+        wq_raw = load_weight("wq_raw", wq)
         ew_tab = load_words("ew_tab", e_words)
-        pb_sb = load_list("pb_sb", pb)
+        pa_sb = load_list("pa_sb", pa)
         with nc.allow_non_contiguous_dma(reason="transition 128 i + p goes to [p, i]"):
             nc.sync.dma_start(disc_sb[:], disc.rearrange("(i p) o -> p (i o)", p=P))
             nc.sync.dma_start(rew_sb[:], rew.rearrange("(i p) o -> p (i o)", p=P))
+        pb_sb = load_list("pb_sb", pb)
         nc.sync.dma_start(bound[:, 0:CONSTS].rearrange("p (h d) -> p h d", d=RUN), pair_row(ku))
         nc.sync.dma_start(kd_sb[:], pair_row(kd))
-        pa_sb = load_list("pa_sb", pa)
 
         ident = keep.tile([P, P], F32, name="ident")
         make_identity(nc, ident[:])
@@ -163,12 +164,12 @@ def tile_picked_yqrdqn_loss_p_kernel(
         result = [keep.tile([P, V], F32, name=f"result{i}") for i in range(TILES)]
 
         def predictions(group, words):
-            acc = product(words, x_bytes, group, wq_mx)
+            acc = product(words, x_bytes[X_ROWS:P, :], group, wq_mx)
             for s in range(2):
                 nc.scalar.activation(y_neg[2 * group + s][:, 0:V], acc[:, s, :], ACT.Copy, scale=-1.0)
 
         def targets(group):
-            acc = product(gather_words(f"e_codes{group}", ew_tab, nxt_sb, group), e_bytes, group, wt_mx)
+            acc = product(gather_words(f"e_codes{group}", ew_tab, nxt_sb, group), e_bytes[E_ROWS:P, :], group, wt_mx)
             for s in range(2):
                 i = 2 * group + s
                 nc.scalar.activation(

from contextlib import ExitStack

import concourse.mybir as mybir
from concourse.masks import make_identity

F32 = mybir.dt.float32
BF16 = mybir.dt.bfloat16
I32 = mybir.dt.int32
U32 = mybir.dt.uint32
U16 = mybir.dt.uint16
U8 = mybir.dt.uint8
FP8X4 = mybir.dt.float8_e4m3fn_x4
ALU = mybir.AluOpType
ACT = mybir.ActivationFunctionType

P = 128
PACK = 4
K = 512
S = 512
V = 256
RUN = 4
HALF = 512
CONSTS = 2 * RUN
TILES = S // P
GROUP = 2 * P
PER_LIST_COLUMN = 16
WINDOW = 520
X_ROWS, E_ROWS = 0, 4
TINY = 1e-30

FLOPS = 2 * 2 * S * K * V

STAGES = [(0, (0, 1)), (1, (0, 1)), (0, (2, 3)), (1, (2,)), (1, (3,))]


def tile_picked_yqrdqn_loss_p_kernel(
    tc, x_words, x_scales, e_words, e_scales, wq, wt, disc, rew, tau, ku, kd, offs, nxt, pa, pb, out
):
    nc = tc.nc
    with ExitStack() as ctx:
        keep = ctx.enter_context(tc.tile_pool(name="keep", bufs=1))
        work = ctx.enter_context(tc.tile_pool(name="work", bufs=4))
        psum = ctx.enter_context(tc.psum_pool(name="psum", bufs=4))

        def load_list(name, src):
            tile = keep.tile(list(src.shape), U16, name=name)
            nc.sync.dma_start(tile[:], src)
            return tile

        def cleared_scale_table(name, src):
            tile = keep.tile([P, src.shape[2]], U8, name=name, tag=name, align_bytes=64)
            nc.gpsimd.memset(tile[:].bitcast(I32), 0)
            return tile

        def load_scales(tile, src, first):
            for r in range(4):
                nc.sync.dma_start(tile[first + r : P : 32, :].bitcast(I32), src[0, r:16:4, :].bitcast(I32))

        def load_words(name, src):
            tile = keep.tile([P, src.shape[2]], I32, name=name, align_bytes=64)
            nc.sync.dma_start(tile[:], src[0].rearrange("p n t -> p (n t)").bitcast(I32))
            return tile

        def load_weight(name, src):
            tile = keep.tile([P, PACK, V], F32, name=name, align_bytes=64)
            nc.sync.dma_start(tile[:], src.rearrange("(p j) v -> p j v", j=PACK))
            return tile

        def pair_row(src):
            return src[0:1, :].rearrange("o (h p d) -> p (o h) d", h=2, d=RUN)

        xs_tab = cleared_scale_table("xs_tab", x_scales)
        es_tab = cleared_scale_table("es_tab", e_scales)
        tau_sb = keep.tile([P, 2, RUN], F32, name="tau_sb")
        kd_sb = keep.tile([P, 2, RUN], F32, name="kd_sb")
        bound = keep.tile([P, 2 * CONSTS], F32, name="bound")
        disc_sb = keep.tile([P, TILES], F32, name="disc_sb")
        rew_sb = keep.tile([P, TILES], F32, name="rew_sb")

        nc.sync.dma_start(tau_sb[:], pair_row(tau))
        offs_sb = load_list("offs_sb", offs)
        load_scales(xs_tab, x_scales, X_ROWS)
        wt_raw = load_weight("wt_raw", wt)
        xw_tab = load_words("xw_tab", x_words)
        nxt_sb = load_list("nxt_sb", nxt)
        load_scales(es_tab, e_scales, E_ROWS)
        wq_raw = load_weight("wq_raw", wq)
        ew_tab = load_words("ew_tab", e_words)
        pa_sb = load_list("pa_sb", pa)
        with nc.allow_non_contiguous_dma(reason="transition 128 i + p goes to [p, i]"):
            nc.sync.dma_start(disc_sb[:], disc.rearrange("(i p) o -> p (i o)", p=P))
            nc.sync.dma_start(rew_sb[:], rew.rearrange("(i p) o -> p (i o)", p=P))
        pb_sb = load_list("pb_sb", pb)
        nc.sync.dma_start(bound[:, 0:CONSTS].rearrange("p (h d) -> p h d", d=RUN), pair_row(ku))
        nc.sync.dma_start(kd_sb[:], pair_row(kd))

        ident = keep.tile([P, P], F32, name="ident")
        make_identity(nc, ident[:])

        tau_f = tau_sb[:].rearrange("p h d -> p (h d)")
        kd_f = kd_sb[:].rearrange("p h d -> p (h d)")
        upper = slice(0, CONSTS)
        lower = slice(CONSTS, 2 * CONSTS)
        root_up = keep.tile([P, CONSTS], F32, name="root_up")
        nc.scalar.activation(root_up[:], tau_f, ACT.Sqrt, scale=0.125, bias=TINY)
        weight = keep.tile([P, 2 * CONSTS], F32, name="weight")
        nc.scalar.activation(weight[:, lower], tau_f, ACT.Copy, scale=-0.25, bias=0.25)
        nc.scalar.activation(weight[:, upper], tau_f, ACT.Copy, scale=0.25)
        root_dn = keep.tile([P, CONSTS], F32, name="root_dn")
        nc.scalar.activation(root_dn[:], weight[:, lower], ACT.Sqrt, scale=0.5, bias=TINY)
        inverse = keep.tile([P, CONSTS], F32, name="inverse")
        nc.vector.reciprocal(inverse[:], root_up[:])
        ratio = keep.tile([P, CONSTS], F32, name="ratio")
        nc.vector.scalar_tensor_tensor(ratio[:], root_dn[:], -1.0, inverse[:], ALU.mult, ALU.mult)
        nc.gpsimd.tensor_scalar(bound[:, lower], kd_f, -1.0, 0.0, ALU.mult, ALU.add)
        slope = keep.tile([P, 2 * CONSTS], F32, name="slope")
        nc.gpsimd.tensor_tensor(slope[:], weight[:], bound[:], ALU.mult)
        knee = keep.tile([P, 2 * CONSTS], F32, name="knee")
        nc.gpsimd.tensor_tensor(knee[:], slope[:], bound[:], ALU.mult)
        shift = keep.tile([P, 2 * CONSTS], F32, name="shift")
        nc.gpsimd.tensor_scalar(shift[:], knee[:], -1.0, 0.0, ALU.mult, ALU.add)

        def entries(lst, first, count):
            return lst[:, first // PER_LIST_COLUMN : (first + count) // PER_LIST_COLUMN]

        def gather_bytes(name, table, lst):
            tile = keep.tile([P, S], U8, name=name, align_bytes=64)
            nc.vector.tensor_copy(tile[:], table[:].indirect(entries(lst, 0, S)))
            return tile

        def gather_words(name, table, lst, group):
            tile = keep.tile([P, GROUP], U32, name=name, align_bytes=64)
            nc.vector.tensor_copy(tile[:], table[:].bitcast(U32).indirect(entries(lst, group * GROUP, GROUP)))
            return tile

        def quantise(name, raw, home):
            grouped = keep.tile([P, V, PACK], BF16, name=name + "_grouped", align_bytes=64)
            nc.scalar.copy(
                grouped[:].rearrange("p (c i) j -> p c j i", i=4),
                raw[:].rearrange("p j (c i) -> p c j i", i=4),
            )
            codes = keep.tile([P, V], U32, name=name + "_codes", tag=home, align_bytes=64)
            scales = keep.tile([P, V], U8, name=name + "_scales", align_bytes=64)
            nc.vector.quantize_mx(codes[:].bitcast(FP8X4), scales[:], grouped[:].rearrange("p v j -> p (v j)"))
            return codes, scales

        def product(words, scale_bytes, group, weights):
            acc = psum.tile([P, 2, V], F32, name="acc", tag="acc")
            for s in range(2):
                first = group * GROUP + s * P
                nc.tensor.matmul_mx(
                    acc[:, s, :],
                    words[:, s * P : (s + 1) * P].bitcast(FP8X4),
                    scale_bytes[:, first : first + P],
                    weights[0][:].bitcast(FP8X4),
                    weights[1][:],
                    start=True,
                    stop=True,
                )
            return acc

        y_neg = [keep.tile([P, WINDOW], F32, name=f"y_neg{i}") for i in range(TILES)]
        h_sb = [keep.tile([P, WINDOW], F32, name=f"h_sb{i}") for i in range(TILES)]
        result = [keep.tile([P, V], F32, name=f"result{i}") for i in range(TILES)]

        def predictions(group, words):
            acc = product(words, x_bytes[X_ROWS:P, :], group, wq_mx)
            for s in range(2):
                nc.scalar.activation(y_neg[2 * group + s][:, 0:V], acc[:, s, :], ACT.Copy, scale=-1.0)

        def targets(group):
            acc = product(gather_words(f"e_codes{group}", ew_tab, nxt_sb, group), e_bytes[E_ROWS:P, :], group, wt_mx)
            for s in range(2):
                i = 2 * group + s
                nc.scalar.activation(
                    h_sb[i][:, 0:V], acc[:, s, :], ACT.Identity, bias=rew_sb[:, i : i + 1], scale=disc_sb[:, i : i + 1]
                )

        shared = [keep.tile([P, HALF], F32, name=f"shared{s}") for s in range(2)]
        swap = [[keep.tile([P, HALF], F32, name=f"swap{a}_{b}") for b in range(2)] for a in range(2)]
        totals = {}

        def part(tiles2, d, width):
            return tiles2[d // 2][:, (d % 2) * width : (d % 2 + 1) * width]

        def differences(k):
            half, tiles = STAGES[k]
            picked = []
            for s, i in enumerate(tiles):
                y_picked = shared[s] if k > 0 else work.tile([P, HALF], F32, name="y_first", bufs=2)
                nc.vector.tensor_copy(y_picked[:], y_neg[i][:].indirect(entries(pa_sb, half * HALF, HALF)))
                picked.append(y_picked)
            td = []
            for s, i in enumerate(tiles):
                diff = work.tile([P, HALF], F32, name="diff")
                nc.vector.tensor_tensor(
                    diff[:], h_sb[i][:].indirect(entries(pb_sb, half * HALF, HALF)), picked[s][:], ALU.add
                )
                td.append(diff)
            return td

        def turn(k, td):
            width = P * len(td)
            for b in range(2):
                bank = psum.tile([P, 2 * width], F32, name="bank", tag="bank")
                for d in (2 * b, 2 * b + 1):
                    for s, diff in enumerate(td):
                        at = (d % 2) * width + s * P
                        nc.tensor.transpose(bank[:, at : at + P], diff[:, d:HALF:RUN], ident[:])
                nc.scalar.copy(swap[k % 2][b][:, 0 : 2 * width], bank[:])

        def linear_terms(k):
            half, tiles = STAGES[k]
            width = P * len(tiles)
            terms = []
            for d in range(RUN):
                for side in range(2):
                    term = work.tile([P, width], F32, name="linear", bufs=4 * RUN)
                    j = side * CONSTS + RUN * half + d
                    nc.scalar.activation(
                        term[:], part(swap[k % 2], d, width), ACT.Relu, bias=shift[:, j : j + 1], scale=slope[:, j : j + 1]
                    )
                    terms.append(term)
            return terms

        def square_terms(k):
            half, tiles = STAGES[k]
            width = P * len(tiles)
            for d in range(RUN):
                j = RUN * half + d
                nc.vector.tensor_scalar(
                    part(shared, d, width), part(swap[k % 2], d, width),
                    bound[:, j : j + 1], bound[:, CONSTS + j : CONSTS + j + 1], ALU.min, ALU.max,
                )
            terms = []
            for d in range(RUN):
                j = RUN * half + d
                clipped = part(shared, d, width)
                folded = part(swap[(k + 1) % 2], d, width)
                nc.vector.scalar_tensor_tensor(folded, clipped, ratio[:, j : j + 1], clipped, ALU.mult, ALU.max)
                term = work.tile([P, width], F32, name="square", bufs=2 * RUN)
                nc.scalar.activation(term[:], folded, ACT.Square, scale=root_up[:, j : j + 1])
                terms.append(term)
            return terms

        def add_up(k, terms):
            half, tiles = STAGES[k]
            for s, i in enumerate(tiles):
                if half == 0:
                    totals[i] = psum.tile([P, V], F32, name="total", tag="acc")
                for at, term in enumerate(terms):
                    nc.tensor.matmul(
                        totals[i][:, half * P : (half + 1) * P], term[:, s * P : (s + 1) * P], ident[:],
                        is_transpose=True, start=(at == 0), stop=(at == len(terms) - 1),
                    )

        def store(k):
            half, tiles = STAGES[k]
            if half == 1:
                for i in tiles:
                    nc.scalar.copy(result[i][:], totals[i][:])
                    nc.sync.dma_start(out[i * P : (i + 1) * P, :], result[i][:])

        x_bytes = gather_bytes("x_bytes", xs_tab, offs_sb)
        wt_mx = quantise("wt", wt_raw, "xs_tab")
        x_codes = [gather_words(f"x_codes{group}", xw_tab, offs_sb, group) for group in range(2)]
        e_bytes = gather_bytes("e_bytes", es_tab, nxt_sb)
        wq_mx = quantise("wq", wq_raw, "es_tab")
        for group in range(2):
            predictions(group, x_codes[group])
        targets(0)
        td = differences(0)
        targets(1)
        for k in range(len(STAGES)):
            turn(k, td)
            linear = linear_terms(k)
            if k + 1 < len(STAGES):
                td = differences(k + 1)
            add_up(k, linear + square_terms(k))
            if k > 0:
                store(k - 1)
        store(len(STAGES) - 1)
